import numpy as np
import ml_dtypes


def mxq(x, axis, fmt="e4m3"):
    dtype, down = {"e4m3": (ml_dtypes.float8_e4m3fn, 7), "e5m2": (ml_dtypes.float8_e5m2, 14)}[fmt]
    v = np.moveaxis(np.asarray(x, np.float32).astype(ml_dtypes.bfloat16).astype(np.float64), axis, -1)
    blocks = v.reshape(v.shape[:-1] + (-1, 32))
    amax = np.abs(blocks).max(-1, keepdims=True)
    byte = np.maximum(np.where(amax > 0, np.frexp(amax)[1] - 1 + 127, 0) - down, 1)
    scale = np.exp2(byte - 127.0)
    codes = (blocks / scale).astype(np.float32).astype(dtype).astype(np.float64)
    return np.moveaxis((codes * scale).reshape(v.shape), -1, axis)


WIDE = False


def mx_kscale(k):
    if not WIDE:
        return np.ones(k)
    levels = np.array([30, -30])
    if k % 512:
        return np.exp2(np.random.permutation(np.resize(levels, k // 32))).repeat(32)
    a = np.empty((k // 512, 16))
    for p in range(k // 512):
        a[p, :8] = np.random.permutation(np.resize(levels, 8))
        for g in range(8):
            far = levels[np.abs(levels - a[p, g]) >= 10]
            a[p, g + 8] = far[np.random.randint(len(far))]
    return np.exp2(a.ravel()).repeat(32)


def f64(x):
    return np.asarray(x).astype(np.float64)


def striped(idx):
    return np.tile(np.asarray(idx).reshape(-1, 16).T, (8, 1)).astype(np.uint16)


def unstriped(offs):
    return offs[:16].T.reshape(-1).astype(np.int64)


E2M1 = np.array([0.0, 0.5, 1.0, 1.5, 2.0, 3.0, 4.0, 6.0, -0.0, -0.5, -1.0, -1.5, -2.0, -3.0, -4.0, -6.0])


def pack_weight(w, fmt):
    k, n = w.shape
    w = f64(np.asarray(w, np.float32).astype(ml_dtypes.bfloat16)).reshape(k // 32, 32, n)
    amax = np.abs(w).max(1)
    if fmt in ("e4m3", "e5m2"):
        byte = np.frexp(amax)[1] - 1 + 127 - (7 if fmt == "e4m3" else 14)
    else:
        mant, ex = np.frexp(amax / 6.0)
        byte = np.where(mant > 0.5, ex, ex - 1) + 127
    byte = np.clip(np.where(amax > 0, byte, 1), 1, 254)
    scaled = (w * np.exp2(127.0 - byte)[:, None, :]).reshape(k, n).astype(np.float32)
    by_word = np.ascontiguousarray(scaled.reshape(k // 512, 128, 4, n).transpose(0, 1, 3, 2))
    if fmt in ("e4m3", "e5m2"):
        words = by_word.astype(ml_dtypes.float8_e4m3fn if fmt == "e4m3" else ml_dtypes.float8_e5m2).view(np.uint8)
    else:
        c = by_word.astype(ml_dtypes.float4_e2m1fn).view(np.uint8) & 0xF
        words = (c[..., 0::2] | (c[..., 1::2] << 4)).reshape(k // 512, 128, 2 * n)
    return np.ascontiguousarray(words), np.ascontiguousarray(byte.astype(np.uint8).reshape(k // 512, 16, n))


def unpack_weight(words, scales, fmt):
    g, _, n = scales.shape
    words = np.ascontiguousarray(words).reshape(g, 128, n, -1)
    if fmt in ("e4m3", "e5m2"):
        vals = words.view(ml_dtypes.float8_e4m3fn if fmt == "e4m3" else ml_dtypes.float8_e5m2).astype(np.float64)
    else:
        nib = np.empty((g, 128, n, 4), np.uint8)
        nib[..., 0::2] = words & 0xF
        nib[..., 1::2] = words >> 4
        vals = E2M1[nib]
    vals = vals * np.repeat(np.exp2(scales.astype(np.float64) - 127.0), 8, axis=1)[..., None]
    return vals.transpose(0, 1, 3, 2).reshape(g * 512, n)


K, T, J, R, C, I, O, N, S = 512, 2048, 256, 512, 512, 128, 128, 256, 1024


def setup_inputs():
    n = np.random.standard_normal
    idx = np.random.permutation(T)[:J]
    idx2 = np.random.permutation(T)[:J]
    idx3 = np.random.permutation(J)[:I]
    idx4 = np.random.permutation(C)[:I]
    idx5 = np.random.permutation(C)[:O]
    idx6 = np.random.permutation(J)[:O]
    idx7 = np.random.permutation(S)[:N]
    fk = mx_kscale(K)
    fr = mx_kscale(R)
    xtp = pack_weight(n((K, T)) / fk[:, None], "e5m2")
    wp = pack_weight(n((K, R)) * 1 / np.sqrt(K) * fk[:, None] * fr, "e2m1")
    vsp = pack_weight(n((R, S)) * 1 / np.sqrt(R) / fr[:, None], "e2m1")
    return {
        "xt_words": xtp[0],
        "xt_scales": xtp[1],
        "w_words": wp[0],
        "w_scales": wp[1],
        "vs_words": vsp[0],
        "vs_scales": vsp[1],
        "offs": striped(idx),
        "offs2": striped(idx2),
        "offs3": striped(idx3),
        "offs4": striped(idx4),
        "offs5": striped(idx5),
        "offs6": striped(idx6),
        "offs7": striped(idx7),
    }


def reference(xt_words, xt_scales, w_words, w_scales, vs_words, vs_scales, offs, offs2, offs3, offs4, offs5, offs6, offs7):
    idx = unstriped(offs)
    idx2 = unstriped(offs2)
    idx3 = unstriped(offs3)
    idx4 = unstriped(offs4)
    idx5 = unstriped(offs5)
    idx6 = unstriped(offs6)
    idx7 = unstriped(offs7)
    xtu = unpack_weight(xt_words, xt_scales, "e5m2")
    wu = unpack_weight(w_words, w_scales, "e2m1")
    vsu = unpack_weight(vs_words, vs_scales, "e2m1")
    xtidxg = xtu[:, idx]
    a = wu.T @ xtidxg
    xtidx2g = xtu[:, idx2]
    b = wu.T @ xtidx2g
    sa = a[:, idx3]
    pw = np.zeros((R, C))
    pw[:, idx4] = sa
    hid = np.maximum(pw[:, idx5], b[:, idx6])
    vsidx7g = vsu[:, idx7]
    hidq = mxq(hid, 0, "e4m3")
    y = vsidx7g.T @ hidq
    return y

@@ -1,0 +1,181 @@
+from contextlib import ExitStack
+
+import concourse.mybir as mybir
+
+K, T, J, R, C, I, O, N, S = 512, 2048, 256, 512, 512, 128, 128, 256, 1024
+FLOPS = 2 * (2 * K * R * J) + 2 * R * N * O
+
+F32 = mybir.dt.float32
+BF16 = mybir.dt.bfloat16
+I32 = mybir.dt.int32
+U32 = mybir.dt.uint32
+U16 = mybir.dt.uint16
+U8 = mybir.dt.uint8
+E4M3X4 = mybir.dt.float8_e4m3fn_x4
+E5M2X4 = mybir.dt.float8_e5m2_x4
+E2M1X4 = mybir.dt.float4_e2m1fn_x4
+COPY = mybir.ActivationFunctionType.Copy
+MAX = mybir.AluOpType.max
+
+P = 128
+PACK = 4
+
+
+def tile_list_pickedposted_tied_store_plain_kernel(
+    tc, xt_words, xt_scales, w_words, w_scales, vs_words, vs_scales, offs, offs2, offs3, offs4, offs5, offs6, offs7, out
+):
+    nc = tc.nc
+
+    def vector_move(dst, src):
+        nc.vector.tensor_copy(dst, src)
+
+    def scalar_move(dst, src):
+        nc.scalar.activation(dst, src, COPY)
+
+    with ExitStack() as ctx:
+        sb = ctx.enter_context(tc.tile_pool(name="sb", bufs=1))
+        ps = ctx.enter_context(tc.psum_pool(name="ps", bufs=1))
+
+        def load_list(src, name):
+            tile = sb.tile(list(src.shape), U16, name=name)
+            nc.sync.dma_start(tile[:], src)
+            return tile
+
+        def zeroed_plane(engine, width, name):
+            plane = sb.tile([P, width], U8, name=name, align_bytes=64)
+            engine.memset(plane[:].bitcast(I32), 0)
+            return plane
+
+        def load_scale_rows(queues, plane, scales):
+            for q, queue in enumerate(queues):
+                queue.dma_start(plane[32 * q : 32 * q + 4, :].bitcast(I32), scales[0, 4 * q : 4 * q + 4, :].bitcast(I32))
+
+        w_plane = zeroed_plane(nc.vector, R, "w_plane")
+        xt_plane = zeroed_plane(nc.vector, T, "xt_plane")
+        vs_plane = zeroed_plane(nc.vector, S, "vs_plane")
+
+        idx = load_list(offs, "idx")
+        w_codes = sb.tile([P, R], U16, name="w_codes", align_bytes=64)
+        nc.scalar.dma_start(w_codes[:].bitcast(I32), w_words[0].bitcast(I32))
+        idx2 = load_list(offs2, "idx2")
+        xt_rows = sb.tile([P, T], U8, name="xt_rows", align_bytes=64)
+        load_scale_rows((nc.scalar, nc.sync, nc.scalar, nc.sync), xt_rows, xt_scales)
+        xt_codes = sb.tile([P, T], U32, name="xt_codes", align_bytes=64)
+        nc.scalar.dma_start(xt_codes[:].bitcast(I32), xt_words[0].rearrange("p c r -> p (c r)").bitcast(I32))
+        load_scale_rows(4 * (nc.sync,), w_plane, w_scales)
+        idx3 = load_list(offs3, "idx3")
+        idx4 = load_list(offs4, "idx4")
+        idx6 = load_list(offs6, "idx6")
+        idx5 = load_list(offs5, "idx5")
+        idx7 = load_list(offs7, "idx7")
+        vs_codes = sb.tile([P, S], U16, name="vs_codes", align_bytes=64)
+        nc.sync.dma_start(vs_codes[:].bitcast(I32), vs_words[0].bitcast(I32))
+        load_scale_rows(4 * (nc.sync,), vs_plane, vs_scales)
+
+        boards = [sb.tile([P, C], F32, name=f"board{t}") for t in range(PACK)]
+        for board in boards:
+            nc.gpsimd.memset(board[:], 0.0)
+
+        w_dealt = sb.tile([P, R], U16, name="w_dealt", align_bytes=64)
+        nc.vector.tensor_copy(
+            w_dealt[:].rearrange("p (t m) -> p t m", t=PACK), w_codes[:].rearrange("p (m t) -> p t m", t=PACK)
+        )
+        for q in range(4):
+            rows = slice(32 * q, 32 * q + 4)
+            nc.vector.tensor_copy(xt_plane[rows, :].bitcast(I32), xt_rows[rows, :].bitcast(I32))
+        xa_scales = sb.tile([P, J], U8, name="xa_scales", align_bytes=64)
+        nc.vector.tensor_copy(xa_scales[:], xt_plane[:].indirect(idx[:]))
+        xa_codes = sb.tile([P, J], U32, name="xa_codes", align_bytes=64)
+        nc.vector.tensor_copy(xa_codes[:], xt_codes[:].indirect(idx[:]))
+        w_dealt_scales = sb.tile([P, R], U8, name="w_dealt_scales", align_bytes=64)
+        nc.gpsimd.tensor_copy(
+            w_dealt_scales[:].rearrange("p (t m) -> p t m", t=PACK), w_plane[:].rearrange("p (m t) -> p t m", t=PACK)
+        )
+        xb_scales = sb.tile([P, J], U8, name="xb_scales", align_bytes=64)
+        nc.vector.tensor_copy(xb_scales[:], xt_plane[:].indirect(idx2[:]))
+        xb_codes = sb.tile([P, J], U32, name="xb_codes", align_bytes=64)
+        nc.vector.tensor_copy(xb_codes[:], xt_codes[:].indirect(idx2[:]))
+
+        def first_product(dst, t, codes, scales):
+            cols = slice(t * P, (t + 1) * P)
+            nc.tensor.matmul_mx(
+                out=dst,
+                lhsT=w_dealt[:, cols].bitcast(E2M1X4),
+                lhsT_scale=w_dealt_scales[:, cols],
+                rhs=codes[:].bitcast(E5M2X4),
+                rhs_scale=scales[:],
+                start=True,
+                stop=True,
+            )
+
+        a0_ps = ps.tile([P, J], F32, name="a0_ps")
+        a1_ps = ps.tile([P, J], F32, name="a1_ps")
+        a23_ps = ps.tile([P, 2, J], F32, name="a23_ps")
+        b01_ps = ps.tile([P, 2, J], F32, name="b01_ps")
+        b23_ps = ps.tile([P, 2, J], F32, name="b23_ps")
+        first_product(a0_ps[:], 0, xa_codes, xa_scales)
+        first_product(a1_ps[:], 1, xa_codes, xa_scales)
+        first_product(a23_ps[:, 0, :], 2, xa_codes, xa_scales)
+        first_product(a23_ps[:, 1, :], 3, xa_codes, xa_scales)
+        first_product(b01_ps[:, 0, :], 0, xb_codes, xb_scales)
+        first_product(b01_ps[:, 1, :], 1, xb_codes, xb_scales)
+        first_product(b23_ps[:, 0, :], 2, xb_codes, xb_scales)
+        first_product(b23_ps[:, 1, :], 3, xb_codes, xb_scales)
+
+        a0 = sb.tile([P, J], F32, name="a0")
+        a1 = sb.tile([P, J], F32, name="a1")
+        a23 = sb.tile([P, 2 * J], F32, name="a23")
+        b01 = sb.tile([P, 2 * J], F32, name="b01")
+        b23 = sb.tile([P, 2 * J], F32, name="b23")
+        a_rows = [a0[:], a1[:], a23[:, 0:J], a23[:, J : 2 * J]]
+        b_rows = [b01[:, 0:J], b01[:, J : 2 * J], b23[:, 0:J], b23[:, J : 2 * J]]
+        seats = [sb.tile([P, I], F32, name=f"seats{t}") for t in range(PACK)]
+        from_board = sb.tile([P, PACK, O], F32, name="from_board")
+        from_b = sb.tile([P, PACK, O], F32, name="from_b")
+        move = [scalar_move, scalar_move, vector_move, vector_move]
+
+        scalar_move(a0[:], a0_ps[:])
+        scalar_move(a1[:], a1_ps[:])
+        vector_move(a23[:], a23_ps[:].rearrange("p h j -> p (h j)"))
+        for t in range(PACK):
+            move[t](seats[t][:], a_rows[t].indirect(idx3[:]))
+        for t in range(PACK):
+            move[t](boards[t][:].indirect(idx4[:]), seats[t][:])
+        scalar_move(b23[:], b23_ps[:].rearrange("p h j -> p (h j)"))
+        scalar_move(b01[:], b01_ps[:].rearrange("p h j -> p (h j)"))
+        for t in range(PACK):
+            move[t](from_board[:, t, :], boards[t][:].indirect(idx5[:]))
+        for t in range(PACK):
+            move[t](from_b[:, t, :], b_rows[t].indirect(idx6[:]))
+
+        vg_codes = sb.tile([P, N], U16, name="vg_codes", align_bytes=64)
+        nc.vector.tensor_copy(vg_codes[:], vs_codes[:].indirect(idx7[:]))
+        vg_scales = sb.tile([P, N], U8, name="vg_scales", align_bytes=64)
+        nc.vector.tensor_copy(vg_scales[:], vs_plane[:].indirect(idx7[:]))
+
+        hid = sb.tile([P, O * PACK], BF16, name="hid", align_bytes=64)
+        nc.vector.tensor_tensor(
+            hid[:].rearrange("p (c i t) -> p c t i", i=4, t=PACK),
+            from_board[:].rearrange("p t (c i) -> p c t i", i=4),
+            from_b[:].rearrange("p t (c i) -> p c t i", i=4),
+            MAX,
+        )
+        hid_codes = sb.tile([P, O], U32, name="hid_codes", align_bytes=64)
+        hid_scales = sb.tile([P, O], U8, name="hid_scales", align_bytes=64)
+        nc.vector.quantize_mx(out=hid_codes[:].bitcast(E4M3X4), scales=hid_scales[:], in_=hid[:])
+
+        for h, (leave, queue) in enumerate(((vector_move, nc.sync), (scalar_move, nc.scalar))):
+            cols = slice(h * P, (h + 1) * P)
+            y_ps = ps.tile([P, O], F32, name=f"y{h}_ps")
+            nc.tensor.matmul_mx(
+                out=y_ps[:],
+                lhsT=vg_codes[:, cols].bitcast(E2M1X4),
+                lhsT_scale=vg_scales[:, cols],
+                rhs=hid_codes[:].bitcast(E4M3X4),
+                rhs_scale=hid_scales[:],
+                start=True,
+                stop=True,
+            )
+            y = sb.tile([P, O], F32, name=f"y{h}")
+            leave(y[:], y_ps[:])
+            queue.dma_start(out[cols, :], y[:])

@@ -42,7 +42,7 @@ def tile_list_pickedposted_tied_store_plain_kernel(
             return tile
 
         def zeroed_plane(engine, width, name):
-            plane = sb.tile([P, width], U8, name=name, align_bytes=64)
+            plane = sb.tile([P, width], U8, name=name, tag=name, align_bytes=64)
             engine.memset(plane[:].bitcast(I32), 0)
             return plane
 
@@ -74,7 +74,7 @@ def tile_list_pickedposted_tied_store_plain_kernel(
 
         boards = [sb.tile([P, C], F32, name=f"board{t}") for t in range(PACK)]
         for board in boards:
-            nc.gpsimd.memset(board[:], 0.0)
+            nc.vector.memset(board[:], 0.0)
 
         w_dealt = sb.tile([P, R], U16, name="w_dealt", align_bytes=64)
         nc.vector.tensor_copy(
@@ -87,21 +87,19 @@ def tile_list_pickedposted_tied_store_plain_kernel(
         nc.vector.tensor_copy(xa_scales[:], xt_plane[:].indirect(idx[:]))
         xa_codes = sb.tile([P, J], U32, name="xa_codes", align_bytes=64)
         nc.vector.tensor_copy(xa_codes[:], xt_codes[:].indirect(idx[:]))
-        w_dealt_scales = sb.tile([P, R], U8, name="w_dealt_scales", align_bytes=64)
-        nc.gpsimd.tensor_copy(
-            w_dealt_scales[:].rearrange("p (t m) -> p t m", t=PACK), w_plane[:].rearrange("p (m t) -> p t m", t=PACK)
-        )
-        xb_scales = sb.tile([P, J], U8, name="xb_scales", align_bytes=64)
-        nc.vector.tensor_copy(xb_scales[:], xt_plane[:].indirect(idx2[:]))
-        xb_codes = sb.tile([P, J], U32, name="xb_codes", align_bytes=64)
+        w_dealt_scales = sb.tile([P, PACK, P], U8, name="w_dealt_scales", align_bytes=64)
+        nc.vector.tensor_copy(w_dealt_scales[:], w_plane[:].rearrange("p (m t) -> p t m", t=PACK))
+        xb_codes = sb.tile([P, J], U32, name="xb_codes", tag="xb_codes", align_bytes=64)
         nc.vector.tensor_copy(xb_codes[:], xt_codes[:].indirect(idx2[:]))
+        xb_scales = sb.tile([P, J], U8, name="xb_scales", tag="xb_scales", align_bytes=64)
+        nc.vector.tensor_copy(xb_scales[:], xt_plane[:].indirect(idx2[:]))
 
         def first_product(dst, t, codes, scales):
             cols = slice(t * P, (t + 1) * P)
             nc.tensor.matmul_mx(
                 out=dst,
                 lhsT=w_dealt[:, cols].bitcast(E2M1X4),
-                lhsT_scale=w_dealt_scales[:, cols],
+                lhsT_scale=w_dealt_scales[:, t, :],
                 rhs=codes[:].bitcast(E5M2X4),
                 rhs_scale=scales[:],
                 start=True,
@@ -111,47 +109,54 @@ def tile_list_pickedposted_tied_store_plain_kernel(
         a0_ps = ps.tile([P, J], F32, name="a0_ps")
         a1_ps = ps.tile([P, J], F32, name="a1_ps")
         a23_ps = ps.tile([P, 2, J], F32, name="a23_ps")
-        b01_ps = ps.tile([P, 2, J], F32, name="b01_ps")
-        b23_ps = ps.tile([P, 2, J], F32, name="b23_ps")
-        first_product(a0_ps[:], 0, xa_codes, xa_scales)
-        first_product(a1_ps[:], 1, xa_codes, xa_scales)
-        first_product(a23_ps[:, 0, :], 2, xa_codes, xa_scales)
-        first_product(a23_ps[:, 1, :], 3, xa_codes, xa_scales)
-        first_product(b01_ps[:, 0, :], 0, xb_codes, xb_scales)
-        first_product(b01_ps[:, 1, :], 1, xb_codes, xb_scales)
-        first_product(b23_ps[:, 0, :], 2, xb_codes, xb_scales)
-        first_product(b23_ps[:, 1, :], 3, xb_codes, xb_scales)
+        b_ps = [ps.tile([P, 2, J], F32, name=f"b{parity}_ps") for parity in range(2)]
+        for t, dst in enumerate((a0_ps[:], a1_ps[:], a23_ps[:, 0, :], a23_ps[:, 1, :])):
+            first_product(dst, t, xa_codes, xa_scales)
+        for t in (1, 3, 0, 2):
+            first_product(b_ps[t % 2][:, t // 2, :], t, xb_codes, xb_scales)
 
         a0 = sb.tile([P, J], F32, name="a0")
         a1 = sb.tile([P, J], F32, name="a1")
         a23 = sb.tile([P, 2 * J], F32, name="a23")
-        b01 = sb.tile([P, 2 * J], F32, name="b01")
-        b23 = sb.tile([P, 2 * J], F32, name="b23")
         a_rows = [a0[:], a1[:], a23[:, 0:J], a23[:, J : 2 * J]]
-        b_rows = [b01[:, 0:J], b01[:, J : 2 * J], b23[:, 0:J], b23[:, J : 2 * J]]
+        b = [sb.tile([P, 2 * J], F32, name=f"b{parity}") for parity in range(2)]
         seats = [sb.tile([P, I], F32, name=f"seats{t}") for t in range(PACK)]
         from_board = sb.tile([P, PACK, O], F32, name="from_board")
         from_b = sb.tile([P, PACK, O], F32, name="from_b")
-        move = [scalar_move, scalar_move, vector_move, vector_move]
+        move = [scalar_move, vector_move, scalar_move, vector_move]
+
+        def seat(t):
+            move[t](seats[t][:], a_rows[t].indirect(idx3[:]))
+
+        def post(t):
+            move[t](boards[t][:].indirect(idx4[:]), seats[t][:])
+
+        def leave_b(parity):
+            scalar_move(b[parity][:], b_ps[parity][:].rearrange("p h j -> p (h j)"))
 
         scalar_move(a0[:], a0_ps[:])
         scalar_move(a1[:], a1_ps[:])
-        vector_move(a23[:], a23_ps[:].rearrange("p h j -> p (h j)"))
-        for t in range(PACK):
-            move[t](seats[t][:], a_rows[t].indirect(idx3[:]))
-        for t in range(PACK):
-            move[t](boards[t][:].indirect(idx4[:]), seats[t][:])
-        scalar_move(b23[:], b23_ps[:].rearrange("p h j -> p (h j)"))
-        scalar_move(b01[:], b01_ps[:].rearrange("p h j -> p (h j)"))
+        seat(0)
+        seat(1)
+        scalar_move(a23[:], a23_ps[:].rearrange("p h j -> p (h j)"))
+        post(0)
+        post(1)
+        seat(2)
+        seat(3)
+        leave_b(1)
+        vg_codes = sb.tile([P, N], U16, name="vg_codes", tag="xb_codes", align_bytes=64)
+        nc.vector.tensor_copy(vg_codes[:], vs_codes[:].indirect(idx7[:]))
+        post(2)
+        post(3)
+        leave_b(0)
+        vg_scales = sb.tile([P, N], U8, name="vg_scales", tag="xb_scales", align_bytes=64)
+        nc.vector.tensor_copy(vg_scales[:], vs_plane[:].indirect(idx7[:]))
         for t in range(PACK):
             move[t](from_board[:, t, :], boards[t][:].indirect(idx5[:]))
-        for t in range(PACK):
-            move[t](from_b[:, t, :], b_rows[t].indirect(idx6[:]))
-
-        vg_codes = sb.tile([P, N], U16, name="vg_codes", align_bytes=64)
-        nc.vector.tensor_copy(vg_codes[:], vs_codes[:].indirect(idx7[:]))
-        vg_scales = sb.tile([P, N], U8, name="vg_scales", align_bytes=64)
-        nc.vector.tensor_copy(vg_scales[:], vs_plane[:].indirect(idx7[:]))
+        for t in (0, 1, 3, 2):
+            half = t // 2
+            pick = scalar_move if t == 0 else vector_move
+            pick(from_b[:, t, :], b[t % 2][:, half * J : (half + 1) * J].indirect(idx6[:]))
 
         hid = sb.tile([P, O * PACK], BF16, name="hid", align_bytes=64)
         nc.vector.tensor_tensor(

@@ -57,11 +57,11 @@ def tile_list_pickedposted_tied_store_plain_kernel(
         idx = load_list(offs, "idx")
         w_codes = sb.tile([P, R], U16, name="w_codes", align_bytes=64)
         nc.scalar.dma_start(w_codes[:].bitcast(I32), w_words[0].bitcast(I32))
-        idx2 = load_list(offs2, "idx2")
         xt_rows = sb.tile([P, T], U8, name="xt_rows", align_bytes=64)
-        load_scale_rows((nc.scalar, nc.sync, nc.scalar, nc.sync), xt_rows, xt_scales)
+        load_scale_rows(4 * (nc.sync,), xt_rows, xt_scales)
+        idx2 = load_list(offs2, "idx2")
         xt_codes = sb.tile([P, T], U32, name="xt_codes", align_bytes=64)
-        nc.scalar.dma_start(xt_codes[:].bitcast(I32), xt_words[0].rearrange("p c r -> p (c r)").bitcast(I32))
+        nc.sync.dma_start(xt_codes[:].bitcast(I32), xt_words[0].rearrange("p c r -> p (c r)").bitcast(I32))
         load_scale_rows(4 * (nc.sync,), w_plane, w_scales)
         idx3 = load_list(offs3, "idx3")
         idx4 = load_list(offs4, "idx4")
@@ -77,7 +77,7 @@ def tile_list_pickedposted_tied_store_plain_kernel(
             nc.vector.memset(board[:], 0.0)
 
         w_dealt = sb.tile([P, R], U16, name="w_dealt", align_bytes=64)
-        nc.vector.tensor_copy(
+        nc.scalar.copy(
             w_dealt[:].rearrange("p (t m) -> p t m", t=PACK), w_codes[:].rearrange("p (m t) -> p t m", t=PACK)
         )
         for q in range(4):
@@ -85,14 +85,15 @@ def tile_list_pickedposted_tied_store_plain_kernel(
             nc.vector.tensor_copy(xt_plane[rows, :].bitcast(I32), xt_rows[rows, :].bitcast(I32))
         xa_scales = sb.tile([P, J], U8, name="xa_scales", align_bytes=64)
         nc.vector.tensor_copy(xa_scales[:], xt_plane[:].indirect(idx[:]))
+        xb_scales = sb.tile([P, J], U8, name="xb_scales", align_bytes=64)
+        nc.vector.tensor_copy(xb_scales[:], xt_plane[:].indirect(idx2[:]))
         xa_codes = sb.tile([P, J], U32, name="xa_codes", align_bytes=64)
         nc.vector.tensor_copy(xa_codes[:], xt_codes[:].indirect(idx[:]))
         w_dealt_scales = sb.tile([P, PACK, P], U8, name="w_dealt_scales", align_bytes=64)
-        nc.vector.tensor_copy(w_dealt_scales[:], w_plane[:].rearrange("p (m t) -> p t m", t=PACK))
-        xb_codes = sb.tile([P, J], U32, name="xb_codes", tag="xb_codes", align_bytes=64)
+        for ts in (slice(0, 2), slice(2, 4)):
+            nc.gpsimd.tensor_copy(w_dealt_scales[:, ts, :], w_plane[:].rearrange("p (m t) -> p t m", t=PACK)[:, ts, :])
+        xb_codes = sb.tile([P, J], U32, name="xb_codes", align_bytes=64)
         nc.vector.tensor_copy(xb_codes[:], xt_codes[:].indirect(idx2[:]))
-        xb_scales = sb.tile([P, J], U8, name="xb_scales", tag="xb_scales", align_bytes=64)
-        nc.vector.tensor_copy(xb_scales[:], xt_plane[:].indirect(idx2[:]))
 
         def first_product(dst, t, codes, scales):
             cols = slice(t * P, (t + 1) * P)
@@ -106,57 +107,37 @@ def tile_list_pickedposted_tied_store_plain_kernel(
                 stop=True,
             )
 
-        a0_ps = ps.tile([P, J], F32, name="a0_ps")
-        a1_ps = ps.tile([P, J], F32, name="a1_ps")
-        a23_ps = ps.tile([P, 2, J], F32, name="a23_ps")
+        a_ps = [ps.tile([P, J], F32, name=f"a{t}_ps") for t in range(PACK)]
         b_ps = [ps.tile([P, 2, J], F32, name=f"b{parity}_ps") for parity in range(2)]
-        for t, dst in enumerate((a0_ps[:], a1_ps[:], a23_ps[:, 0, :], a23_ps[:, 1, :])):
-            first_product(dst, t, xa_codes, xa_scales)
+        for t in range(PACK):
+            first_product(a_ps[t][:], t, xa_codes, xa_scales)
         for t in (1, 3, 0, 2):
             first_product(b_ps[t % 2][:, t // 2, :], t, xb_codes, xb_scales)
 
-        a0 = sb.tile([P, J], F32, name="a0")
-        a1 = sb.tile([P, J], F32, name="a1")
-        a23 = sb.tile([P, 2 * J], F32, name="a23")
-        a_rows = [a0[:], a1[:], a23[:, 0:J], a23[:, J : 2 * J]]
+        a = [sb.tile([P, J], F32, name=f"a{t}") for t in range(PACK)]
         b = [sb.tile([P, 2 * J], F32, name=f"b{parity}") for parity in range(2)]
-        seats = [sb.tile([P, I], F32, name=f"seats{t}") for t in range(PACK)]
+        seats = [sb.tile([P, I], F32, name=f"seats{t}", tag=f"seats{t}", align_bytes=64) for t in range(PACK)]
         from_board = sb.tile([P, PACK, O], F32, name="from_board")
         from_b = sb.tile([P, PACK, O], F32, name="from_b")
         move = [scalar_move, vector_move, scalar_move, vector_move]
 
-        def seat(t):
-            move[t](seats[t][:], a_rows[t].indirect(idx3[:]))
-
-        def post(t):
+        for t in range(PACK):
+            move[t](a[t][:], a_ps[t][:])
+        for t in range(PACK):
+            move[t](seats[t][:], a[t][:].indirect(idx3[:]))
+        for t in range(PACK):
             move[t](boards[t][:].indirect(idx4[:]), seats[t][:])
-
-        def leave_b(parity):
+        for parity in (1, 0):
             scalar_move(b[parity][:], b_ps[parity][:].rearrange("p h j -> p (h j)"))
-
-        scalar_move(a0[:], a0_ps[:])
-        scalar_move(a1[:], a1_ps[:])
-        seat(0)
-        seat(1)
-        scalar_move(a23[:], a23_ps[:].rearrange("p h j -> p (h j)"))
-        post(0)
-        post(1)
-        seat(2)
-        seat(3)
-        leave_b(1)
-        vg_codes = sb.tile([P, N], U16, name="vg_codes", tag="xb_codes", align_bytes=64)
+        vg_codes = sb.tile([P, N], U16, name="vg_codes", tag="seats1", align_bytes=64)
         nc.vector.tensor_copy(vg_codes[:], vs_codes[:].indirect(idx7[:]))
-        post(2)
-        post(3)
-        leave_b(0)
-        vg_scales = sb.tile([P, N], U8, name="vg_scales", tag="xb_scales", align_bytes=64)
+        vg_scales = sb.tile([P, N], U8, name="vg_scales", tag="seats3", align_bytes=64)
         nc.vector.tensor_copy(vg_scales[:], vs_plane[:].indirect(idx7[:]))
         for t in range(PACK):
             move[t](from_board[:, t, :], boards[t][:].indirect(idx5[:]))
-        for t in (0, 1, 3, 2):
+        for t in range(PACK):
             half = t // 2
-            pick = scalar_move if t == 0 else vector_move
-            pick(from_b[:, t, :], b[t % 2][:, half * J : (half + 1) * J].indirect(idx6[:]))
+            move[t](from_b[:, t, :], b[t % 2][:, half * J : (half + 1) * J].indirect(idx6[:]))
 
         hid = sb.tile([P, O * PACK], BF16, name="hid", align_bytes=64)
         nc.vector.tensor_tensor(

from contextlib import ExitStack

import concourse.mybir as mybir

K, T, J, R, C, I, O, N, S = 512, 2048, 256, 512, 512, 128, 128, 256, 1024
FLOPS = 2 * (2 * K * R * J) + 2 * R * N * O

F32 = mybir.dt.float32
BF16 = mybir.dt.bfloat16
I32 = mybir.dt.int32
U32 = mybir.dt.uint32
U16 = mybir.dt.uint16
U8 = mybir.dt.uint8
E4M3X4 = mybir.dt.float8_e4m3fn_x4
E5M2X4 = mybir.dt.float8_e5m2_x4
E2M1X4 = mybir.dt.float4_e2m1fn_x4
COPY = mybir.ActivationFunctionType.Copy
MAX = mybir.AluOpType.max

P = 128
PACK = 4


def tile_list_pickedposted_tied_store_plain_kernel(
    tc, xt_words, xt_scales, w_words, w_scales, vs_words, vs_scales, offs, offs2, offs3, offs4, offs5, offs6, offs7, out
):
    nc = tc.nc

    def vector_move(dst, src):
        nc.vector.tensor_copy(dst, src)

    def scalar_move(dst, src):
        nc.scalar.activation(dst, src, COPY)

    with ExitStack() as ctx:
        sb = ctx.enter_context(tc.tile_pool(name="sb", bufs=1))
        ps = ctx.enter_context(tc.psum_pool(name="ps", bufs=1))

        def load_list(src, name):
            tile = sb.tile(list(src.shape), U16, name=name)
            nc.sync.dma_start(tile[:], src)
            return tile

        def zeroed_plane(engine, width, name):
            plane = sb.tile([P, width], U8, name=name, tag=name, align_bytes=64)
            engine.memset(plane[:].bitcast(I32), 0)
            return plane

        def load_scale_rows(queues, plane, scales):
            for q, queue in enumerate(queues):
                queue.dma_start(plane[32 * q : 32 * q + 4, :].bitcast(I32), scales[0, 4 * q : 4 * q + 4, :].bitcast(I32))

        w_plane = zeroed_plane(nc.vector, R, "w_plane")
        xt_plane = zeroed_plane(nc.vector, T, "xt_plane")
        vs_plane = zeroed_plane(nc.vector, S, "vs_plane")

        idx = load_list(offs, "idx")
        w_codes = sb.tile([P, R], U16, name="w_codes", align_bytes=64)
        nc.scalar.dma_start(w_codes[:].bitcast(I32), w_words[0].bitcast(I32))
        xt_rows = sb.tile([P, T], U8, name="xt_rows", align_bytes=64)
        load_scale_rows(4 * (nc.sync,), xt_rows, xt_scales)
        idx2 = load_list(offs2, "idx2")
        xt_codes = sb.tile([P, T], U32, name="xt_codes", align_bytes=64)
        nc.sync.dma_start(xt_codes[:].bitcast(I32), xt_words[0].rearrange("p c r -> p (c r)").bitcast(I32))
        load_scale_rows(4 * (nc.sync,), w_plane, w_scales)
        idx3 = load_list(offs3, "idx3")
        idx4 = load_list(offs4, "idx4")
        idx6 = load_list(offs6, "idx6")
        idx5 = load_list(offs5, "idx5")
        idx7 = load_list(offs7, "idx7")
        vs_codes = sb.tile([P, S], U16, name="vs_codes", align_bytes=64)
        nc.sync.dma_start(vs_codes[:].bitcast(I32), vs_words[0].bitcast(I32))
        load_scale_rows(4 * (nc.sync,), vs_plane, vs_scales)

        boards = [sb.tile([P, C], F32, name=f"board{t}") for t in range(PACK)]
        for board in boards:
            nc.vector.memset(board[:], 0.0)

        w_dealt = sb.tile([P, R], U16, name="w_dealt", align_bytes=64)
        nc.scalar.copy(
            w_dealt[:].rearrange("p (t m) -> p t m", t=PACK), w_codes[:].rearrange("p (m t) -> p t m", t=PACK)
        )
        for q in range(4):
            rows = slice(32 * q, 32 * q + 4)
            nc.vector.tensor_copy(xt_plane[rows, :].bitcast(I32), xt_rows[rows, :].bitcast(I32))
        xa_scales = sb.tile([P, J], U8, name="xa_scales", align_bytes=64)
        nc.vector.tensor_copy(xa_scales[:], xt_plane[:].indirect(idx[:]))
        xb_scales = sb.tile([P, J], U8, name="xb_scales", align_bytes=64)
        nc.vector.tensor_copy(xb_scales[:], xt_plane[:].indirect(idx2[:]))
        xa_codes = sb.tile([P, J], U32, name="xa_codes", align_bytes=64)
        nc.vector.tensor_copy(xa_codes[:], xt_codes[:].indirect(idx[:]))
        w_dealt_scales = sb.tile([P, PACK, P], U8, name="w_dealt_scales", align_bytes=64)
        for ts in (slice(0, 2), slice(2, 4)):
            nc.gpsimd.tensor_copy(w_dealt_scales[:, ts, :], w_plane[:].rearrange("p (m t) -> p t m", t=PACK)[:, ts, :])
        xb_codes = sb.tile([P, J], U32, name="xb_codes", align_bytes=64)
        nc.vector.tensor_copy(xb_codes[:], xt_codes[:].indirect(idx2[:]))

        def first_product(dst, t, codes, scales):
            cols = slice(t * P, (t + 1) * P)
            nc.tensor.matmul_mx(
                out=dst,
                lhsT=w_dealt[:, cols].bitcast(E2M1X4),
                lhsT_scale=w_dealt_scales[:, t, :],
                rhs=codes[:].bitcast(E5M2X4),
                rhs_scale=scales[:],
                start=True,
                stop=True,
            )

        a_ps = [ps.tile([P, J], F32, name=f"a{t}_ps") for t in range(PACK)]
        b_ps = [ps.tile([P, 2, J], F32, name=f"b{parity}_ps") for parity in range(2)]
        for t in range(PACK):
            first_product(a_ps[t][:], t, xa_codes, xa_scales)
        for t in (1, 3, 0, 2):
            first_product(b_ps[t % 2][:, t // 2, :], t, xb_codes, xb_scales)

        a = [sb.tile([P, J], F32, name=f"a{t}") for t in range(PACK)]
        b = [sb.tile([P, 2 * J], F32, name=f"b{parity}") for parity in range(2)]
        seats = [sb.tile([P, I], F32, name=f"seats{t}", tag=f"seats{t}", align_bytes=64) for t in range(PACK)]
        from_board = sb.tile([P, PACK, O], F32, name="from_board")
        from_b = sb.tile([P, PACK, O], F32, name="from_b")
        move = [scalar_move, vector_move, scalar_move, vector_move]

        for t in range(PACK):
            move[t](a[t][:], a_ps[t][:])
        for t in range(PACK):
            move[t](seats[t][:], a[t][:].indirect(idx3[:]))
        for t in range(PACK):
            move[t](boards[t][:].indirect(idx4[:]), seats[t][:])
        for parity in (1, 0):
            scalar_move(b[parity][:], b_ps[parity][:].rearrange("p h j -> p (h j)"))
        vg_codes = sb.tile([P, N], U16, name="vg_codes", tag="seats1", align_bytes=64)
        nc.vector.tensor_copy(vg_codes[:], vs_codes[:].indirect(idx7[:]))
        vg_scales = sb.tile([P, N], U8, name="vg_scales", tag="seats3", align_bytes=64)
        nc.vector.tensor_copy(vg_scales[:], vs_plane[:].indirect(idx7[:]))
        for t in range(PACK):
            move[t](from_board[:, t, :], boards[t][:].indirect(idx5[:]))
        for t in range(PACK):
            half = t // 2
            move[t](from_b[:, t, :], b[t % 2][:, half * J : (half + 1) * J].indirect(idx6[:]))

        hid = sb.tile([P, O * PACK], BF16, name="hid", align_bytes=64)
        nc.vector.tensor_tensor(
            hid[:].rearrange("p (c i t) -> p c t i", i=4, t=PACK),
            from_board[:].rearrange("p t (c i) -> p c t i", i=4),
            from_b[:].rearrange("p t (c i) -> p c t i", i=4),
            MAX,
        )
        hid_codes = sb.tile([P, O], U32, name="hid_codes", align_bytes=64)
        hid_scales = sb.tile([P, O], U8, name="hid_scales", align_bytes=64)
        nc.vector.quantize_mx(out=hid_codes[:].bitcast(E4M3X4), scales=hid_scales[:], in_=hid[:])

        for h, (leave, queue) in enumerate(((vector_move, nc.sync), (scalar_move, nc.scalar))):
            cols = slice(h * P, (h + 1) * P)
            y_ps = ps.tile([P, O], F32, name=f"y{h}_ps")
            nc.tensor.matmul_mx(
                out=y_ps[:],
                lhsT=vg_codes[:, cols].bitcast(E2M1X4),
                lhsT_scale=vg_scales[:, cols],
                rhs=hid_codes[:].bitcast(E4M3X4),
                rhs_scale=hid_scales[:],
                start=True,
                stop=True,
            )
            y = sb.tile([P, O], F32, name=f"y{h}")
            leave(y[:], y_ps[:])
            queue.dma_start(out[cols, :], y[:])
